import numpy as np, ml_dtypes
CORES = [23,39,55,63,87,103,111,127,18,34,50,58,82,98,106,122]
N = 16
TK = 256
def setup_inputs(rng):
    return {"x": rng.standard_normal((N, 128, TK), dtype=np.float32).astype(ml_dtypes.bfloat16), "w": rng.standard_normal((N, 128, 128), dtype=np.float32).astype(ml_dtypes.bfloat16)}
def setup_inputs_big(rng):
    d = setup_inputs(rng)
    for k in ("x", "w"): d[k] = (d[k].astype(np.float32) * 1024.0).astype(d[k].dtype)
    return d
def setup_inputs_small(rng):
    d = setup_inputs(rng)
    for k in ("x", "w"): d[k] = (d[k].astype(np.float32) * (1 / 1024.0)).astype(d[k].dtype)
    return d
def setup_inputs_apart(rng):
    d = setup_inputs(rng)
    f = (10.0 ** rng.permutation(np.linspace(-1.5, 1.5, N))).astype(np.float32).reshape(N, 1, 1)
    for k in ("x", "w"): d[k] = (d[k].astype(np.float32) * f).astype(d[k].dtype)
    return d
def setup_inputs_neg(rng):
    d = setup_inputs(rng)
    d["x"] = (np.abs(d["x"].astype(np.float32)) * 1048576.0).astype(d["x"].dtype); d["w"] = (-np.abs(d["w"].astype(np.float32))).astype(d["w"].dtype)
    return d
def reference(x, w):
    X, W = x.astype(np.float64), w.astype(np.float64)
    y = np.stack([np.max([W[j].T @ X[r] for j in range(N)], axis=0) for r in range(N)])
    return {"y": y.astype(ml_dtypes.bfloat16)}

@@ -1,0 +1,115 @@
+from concourse.bass import DstId, RemoteDMATransfer
+from concourse.mybir import AluOpType
+
+M = 128
+TK = 256
+NCHIP = 8
+NBANK = 8
+DEFER = 4
+
+SCRATCH = {
+    "wl": ("sbuf", [128, NCHIP * M], "bfloat16"),
+    "xx": ("sbuf", [128, 2 * TK], "bfloat16"),
+    "accp": ("sbuf", [128, TK], "bfloat16"),
+    "acco": ("sbuf", [128, TK], "bfloat16"),
+    "pp": ("sbuf", [128, TK], "bfloat16"),
+    "ysb": ("sbuf", [128, TK], "bfloat16"),
+}
+for _b in range(NBANK):
+    SCRATCH["ps%d" % _b] = ("psum", [128, 512], "float32")
+
+SEMAPHORES = (["ldw", "ldx", "xp", "ppa", "sent", "vp", "vo", "vf", "st"]
+              + ["arr%d" % i for i in range(NCHIP)]
+              + ["mm%d" % j for j in range(2 * NCHIP)])
+
+
+def _bits(mask):
+    return bin(mask).count("1")
+
+
+def rank_program(g, core, T, topo):
+    if T.rank_of(core) is None:
+        return
+    S = T.sem
+    chips = sorted({topo.chip(c) for c in T.cores})
+    n = len(chips)
+    me = chips.index(topo.chip(core))
+    partner = [c for c in T.cores if c != core and topo.chip(c) == topo.chip(core)][0]
+    peer = {chips.index(topo.chip(c)): c for c in T.cores
+            if topo.chip(c) != topo.chip(core) and topo.die(c) == topo.die(core) and topo.may_write(core, c)}
+
+    def slot(i):
+        return T.wl[:, i * M:(i + 1) * M]
+
+    def did(c):
+        rid, pid, _ = topo.addr(c)
+        return DstId(rid=rid, pnc=pid)
+
+    on = topo.mask(core, partner)
+    off = on
+    for c in peer.values():
+        off &= topo.mask(core, c)
+    rest = on & ~off
+    xmask = rest if rest else on
+    prid, ppid, _ = topo.addr(partner)
+
+    x_own = T.xx[:, 0:TK]
+    x_par = T.xx[:, TK:2 * TK]
+
+    g.sync.dma_start(slot(me), T.w[:]).then_inc(S.ldw, 16)
+    g.scalar.dma_start(x_own, T.x[:]).then_inc(S.ldx, 16)
+
+    g.wait_ge(S.ldw, 16)
+    order = [(me + t) % n for t in range(1, n)]
+    g.remote_dma_fused(
+        [RemoteDMATransfer(dst_ids=[did(peer[i]) for i in order], dma_engine_mask=off,
+                           remote_sem=S["arr%d" % me], srcs=[slot(me)], dsts=[slot(me) for _ in order], alu_op=0)],
+        local_sem=S.sent)
+    g.wait_ge(S.ldx, 16)
+    g.remote_dma(x_par, x_own, S.xp, S.sent, ppid, prid, xmask)
+
+    arrivals = [(me - t) % n for t in range(1, n)]
+    early, late = arrivals[:n - 1 - DEFER], arrivals[n - 1 - DEFER:]
+    jobs = [("O", me), ("P", me)]
+    for i in early:
+        jobs += [("P", i), ("O", i)]
+    jobs += [("P", i) for i in late] + [("O", i) for i in late]
+    chain = {"P": S.vp, "O": S.vo}
+    place, cnt = [], {"P": 0, "O": 0}
+    for kind, _ in jobs:
+        cnt[kind] += 1
+        place.append(cnt[kind])
+    bank = [T["ps%d" % (j % NBANK)] for j in range(len(jobs))]
+
+    seen = set()
+    for j, (kind, i) in enumerate(jobs):
+        for key, sem, val in ((("w", i), S.ldw if i == me else S["arr%d" % i], 16 if i == me else _bits(off)),
+                              (("x", kind), S.ldx if kind == "O" else S.xp, 16 if kind == "O" else _bits(xmask))):
+            if key not in seen:
+                seen.add(key)
+                g.tensor.wait_ge(sem, val)
+        if j >= NBANK:
+            g.tensor.wait_ge(chain[jobs[j - NBANK][0]], place[j - NBANK])
+        g.tensor.matmul(bank[j][:, 0:TK], slot(i), x_own if kind == "O" else x_par, True, True).then_inc(S["mm%d" % j], 1)
+
+    acc = {"P": T.accp, "O": T.acco}
+    last_o = max(j for j, (kind, _) in enumerate(jobs) if kind == "O")
+    for j, (kind, i) in enumerate(jobs):
+        g.vector.wait_ge(S["mm%d" % j], 1)
+        if place[j] == 1:
+            g.vector.tensor_copy(acc[kind][:], bank[j][:, 0:TK]).then_inc(chain[kind], 1)
+        else:
+            g.vector.wait_ge(chain[kind], place[j] - 1)
+            out = bank[j][:, TK:2 * TK] if j == last_o else acc[kind][:]
+            g.vector.tensor_tensor(out, bank[j][:, 0:TK], acc[kind][:], AluOpType.max).then_inc(chain[kind], 1)
+    g.vector.wait_ge(S.vo, n)
+    g.vector.wait_ge(S.ppa, _bits(on))
+    g.vector.tensor_tensor(T.ysb[:], bank[last_o][:, TK:2 * TK], T.pp[:], AluOpType.max).then_inc(S.vf, 1)
+
+    g.wait_ge(S.vp, n)
+    g.remote_dma(T.pp[:], T.accp[:], S.ppa, S.sent, ppid, prid, on)
+    g.wait_ge(S.sent, _bits(off) + _bits(xmask) + _bits(on))
+
+    g.sync.wait_ge(S.vf, 1)
+    g.sync.dma_start(T.y[:], T.ysb[:]).then_inc(S.st, 16)
+    g.sync.wait_ge(S.st, 16)

@@ -5,10 +5,13 @@ M = 128
 TK = 256
 NCHIP = 8
 NBANK = 8
-DEFER = 4
+NH = 2
+HW = TK // NH
+BACK = NBANK // NH
+ORDER = "O0 O1 P0 P1 P2 O2 P3 O3 P4 O4 P5 P6 O5 O6 O7 O8"
 
 SCRATCH = {
-    "wl": ("sbuf", [128, NCHIP * M], "bfloat16"),
+    "wl": ("sbuf", [128, (NCHIP + 1) * M], "bfloat16"),
     "xx": ("sbuf", [128, 2 * TK], "bfloat16"),
     "accp": ("sbuf", [128, TK], "bfloat16"),
     "acco": ("sbuf", [128, TK], "bfloat16"),
@@ -18,9 +21,10 @@ SCRATCH = {
 for _b in range(NBANK):
     SCRATCH["ps%d" % _b] = ("psum", [128, 512], "float32")
 
-SEMAPHORES = (["ldw", "ldx", "xp", "ppa", "sent", "vp", "vo", "vf", "st"]
+SEMAPHORES = (["ldw", "ldx", "xp", "ppa", "sent", "vf", "st", "crs"]
+              + ["vP%d" % h for h in range(NH)] + ["vO%d" % h for h in range(NH)]
               + ["arr%d" % i for i in range(NCHIP)]
-              + ["mm%d" % j for j in range(2 * NCHIP)])
+              + ["mm%d_%d" % (j, h) for j in range(2 * NCHIP) for h in range(NH)])
 
 
 def _bits(mask):
@@ -37,6 +41,8 @@ def rank_program(g, core, T, topo):
     partner = [c for c in T.cores if c != core and topo.chip(c) == topo.chip(core)][0]
     peer = {chips.index(topo.chip(c)): c for c in T.cores
             if topo.chip(c) != topo.chip(core) and topo.die(c) == topo.die(core) and topo.may_write(core, c)}
+    cross = {chips.index(topo.chip(c)): c for c in T.cores
+             if topo.chip(c) != topo.chip(core) and topo.die(c) != topo.die(core) and topo.may_write(core, c)}
 
     def slot(i):
         return T.wl[:, i * M:(i + 1) * M]
@@ -47,7 +53,7 @@ def rank_program(g, core, T, topo):
 
     on = topo.mask(core, partner)
     off = on
-    for c in peer.values():
+    for c in list(peer.values()) + list(cross.values()):
         off &= topo.mask(core, c)
     rest = on & ~off
     xmask = rest if rest else on
@@ -67,49 +73,68 @@ def rank_program(g, core, T, topo):
         local_sem=S.sent)
     g.wait_ge(S.ldx, 16)
     g.remote_dma(x_par, x_own, S.xp, S.sent, ppid, prid, xmask)
+    crid, cpid, _ = topo.addr(cross[order[-1]])
+    g.remote_dma(slot(n), slot(me), S.crs, S.sent, cpid, crid, off)
 
-    arrivals = [(me - t) % n for t in range(1, n)]
-    early, late = arrivals[:n - 1 - DEFER], arrivals[n - 1 - DEFER:]
-    jobs = [("O", me), ("P", me)]
-    for i in early:
-        jobs += [("P", i), ("O", i)]
-    jobs += [("P", i) for i in late] + [("O", i) for i in late]
-    chain = {"P": S.vp, "O": S.vo}
+    jobs = [(a[0], int(a[1:])) for a in ORDER.split()]
+
+    def src(t):
+        if t == 0:
+            return slot(me), S.ldw, 16
+        if t < n:
+            i = (me - t) % n
+            return slot(i), S["arr%d" % i], _bits(off)
+        return slot(n), S.crs, _bits(off)
+
+    def chain(kind, h):
+        return S["v%s%d" % (kind, h)]
+
+    def bank(j, h):
+        return T["ps%d" % ((NH * j + h) % NBANK)]
+
     place, cnt = [], {"P": 0, "O": 0}
     for kind, _ in jobs:
         cnt[kind] += 1
         place.append(cnt[kind])
-    bank = [T["ps%d" % (j % NBANK)] for j in range(len(jobs))]
 
     seen = set()
-    for j, (kind, i) in enumerate(jobs):
-        for key, sem, val in ((("w", i), S.ldw if i == me else S["arr%d" % i], 16 if i == me else _bits(off)),
+    for j, (kind, t) in enumerate(jobs):
+        w_ap, w_sem, w_val = src(t)
+        for key, sem, val in ((("w", t), w_sem, w_val),
                               (("x", kind), S.ldx if kind == "O" else S.xp, 16 if kind == "O" else _bits(xmask))):
             if key not in seen:
                 seen.add(key)
                 g.tensor.wait_ge(sem, val)
-        if j >= NBANK:
-            g.tensor.wait_ge(chain[jobs[j - NBANK][0]], place[j - NBANK])
-        g.tensor.matmul(bank[j][:, 0:TK], slot(i), x_own if kind == "O" else x_par, True, True).then_inc(S["mm%d" % j], 1)
+        x0 = 0 if kind == "O" else TK
+        for h in range(NH):
+            if j >= BACK:
+                g.tensor.wait_ge(chain(jobs[j - BACK][0], h), place[j - BACK])
+            g.tensor.matmul(bank(j, h)[:, 0:HW], w_ap, T.xx[:, x0 + h * HW:x0 + (h + 1) * HW],
+                            True, True).then_inc(S["mm%d_%d" % (j, h)], 1)
 
     acc = {"P": T.accp, "O": T.acco}
     last_o = max(j for j, (kind, _) in enumerate(jobs) if kind == "O")
-    for j, (kind, i) in enumerate(jobs):
-        g.vector.wait_ge(S["mm%d" % j], 1)
-        if place[j] == 1:
-            g.vector.tensor_copy(acc[kind][:], bank[j][:, 0:TK]).then_inc(chain[kind], 1)
-        else:
-            g.vector.wait_ge(chain[kind], place[j] - 1)
-            out = bank[j][:, TK:2 * TK] if j == last_o else acc[kind][:]
-            g.vector.tensor_tensor(out, bank[j][:, 0:TK], acc[kind][:], AluOpType.max).then_inc(chain[kind], 1)
-    g.vector.wait_ge(S.vo, n)
+    for j, (kind, t) in enumerate(jobs):
+        for h in range(NH):
+            a, b = h * HW, (h + 1) * HW
+            g.vector.wait_ge(S["mm%d_%d" % (j, h)], 1)
+            if place[j] == 1:
+                g.vector.tensor_copy(acc[kind][:, a:b], bank(j, h)[:, 0:HW]).then_inc(chain(kind, h), 1)
+            else:
+                g.vector.wait_ge(chain(kind, h), place[j] - 1)
+                out = bank(j, h)[:, HW:2 * HW] if j == last_o else acc[kind][:, a:b]
+                g.vector.tensor_tensor(out, bank(j, h)[:, 0:HW], acc[kind][:, a:b], AluOpType.max).then_inc(chain(kind, h), 1)
     g.vector.wait_ge(S.ppa, _bits(on))
-    g.vector.tensor_tensor(T.ysb[:], bank[last_o][:, TK:2 * TK], T.pp[:], AluOpType.max).then_inc(S.vf, 1)
+    for h in range(NH):
+        a, b = h * HW, (h + 1) * HW
+        g.vector.wait_ge(chain("O", h), cnt["O"])
+        g.vector.tensor_tensor(T.ysb[:, a:b], bank(last_o, h)[:, HW:2 * HW], T.pp[:, a:b], AluOpType.max).then_inc(S.vf, 1)
 
-    g.wait_ge(S.vp, n)
+    for h in range(NH):
+        g.wait_ge(chain("P", h), cnt["P"])
     g.remote_dma(T.pp[:], T.accp[:], S.ppa, S.sent, ppid, prid, on)
-    g.wait_ge(S.sent, _bits(off) + _bits(xmask) + _bits(on))
+    g.wait_ge(S.sent, 2 * _bits(off) + _bits(xmask) + _bits(on))
 
-    g.sync.wait_ge(S.vf, 1)
+    g.sync.wait_ge(S.vf, NH)
     g.sync.dma_start(T.y[:], T.ysb[:]).then_inc(S.st, 16)
     g.sync.wait_ge(S.st, 16)

from concourse.bass import DstId, RemoteDMATransfer
from concourse.mybir import AluOpType

M = 128
TK = 256
NCHIP = 8
NBANK = 8
NH = 2
HW = TK // NH
BACK = NBANK // NH
ORDER = "O0 O1 P0 P1 P2 O2 P3 O3 P4 O4 P5 P6 O5 O6 O7 O8"

SCRATCH = {
    "wl": ("sbuf", [128, (NCHIP + 1) * M], "bfloat16"),
    "xx": ("sbuf", [128, 2 * TK], "bfloat16"),
    "accp": ("sbuf", [128, TK], "bfloat16"),
    "acco": ("sbuf", [128, TK], "bfloat16"),
    "pp": ("sbuf", [128, TK], "bfloat16"),
    "ysb": ("sbuf", [128, TK], "bfloat16"),
}
for _b in range(NBANK):
    SCRATCH["ps%d" % _b] = ("psum", [128, 512], "float32")

SEMAPHORES = (["ldw", "ldx", "xp", "ppa", "sent", "vf", "st", "crs"]
              + ["vP%d" % h for h in range(NH)] + ["vO%d" % h for h in range(NH)]
              + ["arr%d" % i for i in range(NCHIP)]
              + ["mm%d_%d" % (j, h) for j in range(2 * NCHIP) for h in range(NH)])


def _bits(mask):
    return bin(mask).count("1")


def rank_program(g, core, T, topo):
    if T.rank_of(core) is None:
        return
    S = T.sem
    chips = sorted({topo.chip(c) for c in T.cores})
    n = len(chips)
    me = chips.index(topo.chip(core))
    partner = [c for c in T.cores if c != core and topo.chip(c) == topo.chip(core)][0]
    peer = {chips.index(topo.chip(c)): c for c in T.cores
            if topo.chip(c) != topo.chip(core) and topo.die(c) == topo.die(core) and topo.may_write(core, c)}
    cross = {chips.index(topo.chip(c)): c for c in T.cores
             if topo.chip(c) != topo.chip(core) and topo.die(c) != topo.die(core) and topo.may_write(core, c)}

    def slot(i):
        return T.wl[:, i * M:(i + 1) * M]

    def did(c):
        rid, pid, _ = topo.addr(c)
        return DstId(rid=rid, pnc=pid)

    on = topo.mask(core, partner)
    off = on
    for c in list(peer.values()) + list(cross.values()):
        off &= topo.mask(core, c)
    rest = on & ~off
    xmask = rest if rest else on
    prid, ppid, _ = topo.addr(partner)

    x_own = T.xx[:, 0:TK]
    x_par = T.xx[:, TK:2 * TK]

    g.sync.dma_start(slot(me), T.w[:]).then_inc(S.ldw, 16)
    g.scalar.dma_start(x_own, T.x[:]).then_inc(S.ldx, 16)

    g.wait_ge(S.ldw, 16)
    order = [(me + t) % n for t in range(1, n)]
    g.remote_dma_fused(
        [RemoteDMATransfer(dst_ids=[did(peer[i]) for i in order], dma_engine_mask=off,
                           remote_sem=S["arr%d" % me], srcs=[slot(me)], dsts=[slot(me) for _ in order], alu_op=0)],
        local_sem=S.sent)
    g.wait_ge(S.ldx, 16)
    g.remote_dma(x_par, x_own, S.xp, S.sent, ppid, prid, xmask)
    crid, cpid, _ = topo.addr(cross[order[-1]])
    g.remote_dma(slot(n), slot(me), S.crs, S.sent, cpid, crid, off)

    jobs = [(a[0], int(a[1:])) for a in ORDER.split()]

    def src(t):
        if t == 0:
            return slot(me), S.ldw, 16
        if t < n:
            i = (me - t) % n
            return slot(i), S["arr%d" % i], _bits(off)
        return slot(n), S.crs, _bits(off)

    def chain(kind, h):
        return S["v%s%d" % (kind, h)]

    def bank(j, h):
        return T["ps%d" % ((NH * j + h) % NBANK)]

    place, cnt = [], {"P": 0, "O": 0}
    for kind, _ in jobs:
        cnt[kind] += 1
        place.append(cnt[kind])

    seen = set()
    for j, (kind, t) in enumerate(jobs):
        w_ap, w_sem, w_val = src(t)
        for key, sem, val in ((("w", t), w_sem, w_val),
                              (("x", kind), S.ldx if kind == "O" else S.xp, 16 if kind == "O" else _bits(xmask))):
            if key not in seen:
                seen.add(key)
                g.tensor.wait_ge(sem, val)
        x0 = 0 if kind == "O" else TK
        for h in range(NH):
            if j >= BACK:
                g.tensor.wait_ge(chain(jobs[j - BACK][0], h), place[j - BACK])
            g.tensor.matmul(bank(j, h)[:, 0:HW], w_ap, T.xx[:, x0 + h * HW:x0 + (h + 1) * HW],
                            True, True).then_inc(S["mm%d_%d" % (j, h)], 1)

    acc = {"P": T.accp, "O": T.acco}
    last_o = max(j for j, (kind, _) in enumerate(jobs) if kind == "O")
    for j, (kind, t) in enumerate(jobs):
        for h in range(NH):
            a, b = h * HW, (h + 1) * HW
            g.vector.wait_ge(S["mm%d_%d" % (j, h)], 1)
            if place[j] == 1:
                g.vector.tensor_copy(acc[kind][:, a:b], bank(j, h)[:, 0:HW]).then_inc(chain(kind, h), 1)
            else:
                g.vector.wait_ge(chain(kind, h), place[j] - 1)
                out = bank(j, h)[:, HW:2 * HW] if j == last_o else acc[kind][:, a:b]
                g.vector.tensor_tensor(out, bank(j, h)[:, 0:HW], acc[kind][:, a:b], AluOpType.max).then_inc(chain(kind, h), 1)
    g.vector.wait_ge(S.ppa, _bits(on))
    for h in range(NH):
        a, b = h * HW, (h + 1) * HW
        g.vector.wait_ge(chain("O", h), cnt["O"])
        g.vector.tensor_tensor(T.ysb[:, a:b], bank(last_o, h)[:, HW:2 * HW], T.pp[:, a:b], AluOpType.max).then_inc(S.vf, 1)

    for h in range(NH):
        g.wait_ge(chain("P", h), cnt["P"])
    g.remote_dma(T.pp[:], T.accp[:], S.ppa, S.sent, ppid, prid, on)
    g.wait_ge(S.sent, 2 * _bits(off) + _bits(xmask) + _bits(on))

    g.sync.wait_ge(S.vf, NH)
    g.sync.dma_start(T.y[:], T.ysb[:]).then_inc(S.st, 16)
    g.sync.wait_ge(S.st, 16)
